import numpy as np, ml_dtypes
CORES = [2,3,42,43,82,83,122,123]
N = 8
BF = ml_dtypes.bfloat16
B, LE, LP, M, ST, RO, TH = 1984, 160, 96, 128, 2, 3, 32768
E = RO * LE + LP
W = B + RO * ST * M
def parts(rng):
    c = (65536 * rng.random((N, 8, 16, B)) * np.exp2(-1.0 * rng.integers(0, 7, (N, 8, 1, B)))).astype(np.int64)
    return c, rng.integers(0, B, (N, 8, 16, B))
def starts(rng, c, share):
    e = np.where(rng.random((N, 8, 1, E)) < share, rng.integers(0, 3, (N, 8, 1, E)), rng.integers(4, 9, (N, 8, 1, E)))
    c[..., B - E:] = (65536 * rng.random((N, 8, 16, E)) * np.exp2(-1.0 * e)).astype(np.int64)
    return c
def pack(c, s):
    return {"c0": np.ascontiguousarray(c.reshape(N, 128, B)).astype(np.int32), "s0": np.ascontiguousarray(s.reshape(N, 128, B)).astype(np.int32)}
def setup_inputs(rng):
    c, s = parts(rng)
    return pack(starts(rng, c, rng.choice(np.array([0.4, 0.7, 0.9, 1.0]), (N, 8, 1, 1))), s)
def setup_inputs_room(rng):
    c, s = parts(rng); c = starts(rng, c, 0.8)
    for q in range(N):
        for g in range(8):
            n = int(rng.choice(np.array([0, 1, M - 1, M, M + 1, LE]))); z = int(rng.choice(np.array([0, 1, LP - 1, LP, LP + 1, M])))
            if q == 0: n = (M, M + 1, LE, M - 1, M, 1, 0, M)[g]; z = (LP, LP + 1, M, LP - 1, 0, 1, 0, 1)[g]
            live = min(n, M); z = min(z, live)
            pool = rng.permutation(B - E); ch = pool[:ST * LE].reshape(ST, LE); nil = pool[ST * LE:ST * LE + 64]; ent = B - E + np.arange(LE)
            who = np.sort(rng.permutation(LE)[:n]); drop = np.delete(who[:M], rng.permutation(live)[:z])
            c[q, g][:, ent] = 0; c[q, g][:, ent[who]] = rng.integers(30000, 65536, (16, n))
            c[q, g][:, ch.reshape(-1)] = rng.integers(20000, 65536, (16, ST * LE)); c[q, g][:, nil] = 0
            c[q, g][:, ch[ST - 1][drop]] = 0
            prev = ent
            for st in range(ST):
                own = np.where(rng.random((16, LE)) < 0.4, ch[st][None, :], rng.choice(nil, (16, LE)))
                own[rng.integers(0, 16, LE), np.arange(LE)] = ch[st]
                s[q, g][:, prev] = own; prev = ch[st]
    return pack(c, s)
def setup_inputs_ties(rng):
    c, s = parts(rng); u = TH // 16
    one = (np.arange(16).reshape(1, 1, 16, 1) == rng.integers(0, 16, (N, 8, 1, B))).astype(np.int64)
    full = rng.random((N, 8, 1, B)) < np.array([0.05, 0.1, 0.2, 0.5, 0.05, 0.1, 0.2, 0.5]).reshape(1, 8, 1, 1)
    c = np.where(full, u, u - one); c = np.where(rng.random((N, 8, 1, B)) < 0.1, 0, c)
    big = rng.random((N, 8, 1, B)) < 0.1; big[:, :4] = False; c = np.where(big, 65535, c)
    c[..., B - E:] = np.where(rng.random((N, 8, 1, E)) < 0.7, 65535, u - one[..., B - E:] * rng.integers(0, 2, (N, 8, 1, E)))
    s[:, :4] = rng.integers(0, B - E, (N, 4, 16, B))
    return pack(c, s)
def setup_inputs_alike(rng):
    c, s = parts(rng); c = starts(rng, c, 0.85)
    for q in range(N):
        for g in range(8):
            h = (1, 2, 17, 64, 160, 300, B // 4, B)[(g + q) % 8]
            s[q, g] = rng.permutation(B)[:h][rng.integers(0, h, (16, B))]
    s = np.where(rng.random(s.shape) < 0.1, np.arange(B), s)
    ends = rng.random(s.shape) < 0.05; ends[:, ::2] = False
    s = np.where(ends, rng.choice(np.array([0, B - 1]), s.shape), s); c[:, 1::2, :, 0] = 65535; c[:, 1::2, :, B - 1] = 65535
    return pack(c, s)
def setup_inputs_links(rng):
    c, s = parts(rng); c = c >> 3; c = starts(rng, c, 0.9)
    near = rng.random(s.shape) < 0.5; near[:, ::2] = True
    return pack(c, np.where(near, rng.integers(B - E, B, s.shape), s))
def setup_inputs_spread(rng):
    c, s = parts(rng); lo = rng.choice(np.array([0.0, 6.0, 10.0]), (N, 8, 1, 1))
    c = np.minimum((np.exp2(lo + (16.0 - lo) * rng.random((N, 8, 1, B))) * rng.random((N, 8, 16, B))).astype(np.int64), 65535)
    c[:, :, :, B - E::7] = rng.integers(0, 65536, c[:, :, :, B - E::7].shape)
    v = rng.random((N, 4, 16, B)); s[:, 1::2] = np.minimum((B * v * v).astype(np.int64), B - 1)
    return pack(c, s)
def check_inputs(d):
    bad = []
    for k, hi in (("c0", 65535), ("s0", B - 1)):
        if np.min(d[k]) < 0 or np.max(d[k]) > hi: bad.append("range of " + k)
    return bad
def reference(c0, s0):
    C = np.zeros((N, 8, 16, W), np.int64); S = np.zeros((N, 8, 16, W), np.int64)
    C[..., :B] = c0.reshape(N, 8, 16, B); S[..., :B] = s0.reshape(N, 8, 16, B)
    port = np.zeros((N, 8, 16, LP), np.int64)
    for rnd in range(RO):
        x = np.concatenate([B - E + rnd * LE + np.arange(LE), B - LP + np.arange(LP)])
        c = np.concatenate([C[..., x[:LE]], port], axis=3)
        for st in range(ST):
            b = B + (rnd * ST + st) * M
            sx = S[..., x]
            score = np.stack([np.add.reduce(np.minimum(c, np.take_along_axis(C, sx[:, :, i][:, :, None, :], 3)), axis=2) for i in range(16)], axis=2)
            k = np.argmax(score, axis=2); best = np.max(score, axis=2)
            y = np.take_along_axis(sx, k[:, :, None, :], 2)[:, :, 0]
            for a in range(N):
                for g in range(8):
                    l = np.flatnonzero(best[a, g] >= TH)
                    l = l[np.sort(np.unique(y[a, g, l], return_index=True)[1])][:M]
                    n = b + np.arange(l.size); yy = y[a, g, l]
                    m = np.minimum(c[a, g][:, l], C[a, g][:, yy]); old = S[a, g][:, yy]
                    C[a, g][:, yy] -= m
                    C[a, g][:, n] = m; S[a, g][:, n] = old
                    S[a, g][k[a, g, l], x[l]] = n
            x = b + np.arange(M); c = np.array(C[..., b:b + M])
        port = np.roll(c[..., :LP], 1, axis=0)
    return {"yc": C.reshape(N, 128, W).astype(np.float32), "ys": np.ascontiguousarray(S[..., B - E:]).reshape(N, 128, W - B + E).astype(np.float32)}

@@ -1,0 +1,357 @@
+from concourse.mybir import dt, AluOpType, ActivationFunctionType
+
+PAD = 136
+NV = 2752
+COL = PAD + NV
+DSZ = 368
+CW = COL + 2 * DSZ
+SW = COL + DSZ
+THR = 524287.5
+
+F32, BF, I32, U16 = "float32", "bfloat16", "int32", "uint16"
+SCRATCH = {
+    "C": ("sbuf", [128, CW], F32), "S": ("sbuf", [128, SW], F32),
+    "CL": ("sbuf", [128, 1984], I32), "SL": ("sbuf", [128, 1984], I32),
+    "S16E": ("sbuf", [128, 576], U16), "S16N": ("sbuf", [128, 128], U16),
+    "P1": ("sbuf", [128, 96], F32), "P2": ("sbuf", [128, 96], F32),
+    "CX": ("sbuf", [128, 4096], F32), "MN": ("sbuf", [128, 4096], F32),
+    "REPI": ("sbuf", [128, 64], I32), "REPL": ("sbuf", [128, 64], U16),
+    "PI": ("sbuf", [128, 1], I32), "PA": ("sbuf", [128, 1], I32), "PM": ("sbuf", [128, 1], F32),
+    "K8": ("sbuf", [128, 1], F32), "IR": ("sbuf", [128, 128], F32),
+    "ONEF": ("sbuf", [128, 128], F32), "ONEB": ("sbuf", [128, 128], BF),
+    "IDF": ("sbuf", [128, 128], F32), "ID1": ("sbuf", [128, 128], F32), "IDB": ("sbuf", [128, 128], BF),
+    "BA": ("sbuf", [128, 128], BF), "BONES": ("sbuf", [128, 128], BF),
+    "TC": ("sbuf", [128, 16], F32), "EQ": ("sbuf", [128, 16], F32),
+    "TRI": ("sbuf", [128, 2048], BF), "SEL": ("sbuf", [128, 2048], BF),
+    "SW0": ("sbuf", [128, 8], F32), "SW1": ("sbuf", [128, 8], F32), "SW16": ("sbuf", [128, 8], F32),
+    "Q0": ("sbuf", [128, 8], F32), "Q1": ("sbuf", [128, 8], F32),
+    "KB": ("sbuf", [128, 128], BF), "PB": ("sbuf", [128, 128], F32), "RST": ("sbuf", [128, 128], F32),
+    "Z3": ("sbuf", [128, 144], F32), "ZERO": ("sbuf", [128, 256], F32),
+    "SLOT": ("sbuf", [128, 16], F32), "DUMPY": ("sbuf", [128, 16], F32), "DUMPN": ("sbuf", [128, 16], F32),
+    "F0": ("sbuf", [128, 128], F32), "F1": ("sbuf", [128, 128], F32),
+    "EM0": ("sbuf", [128, 128], F32), "EM1": ("sbuf", [128, 128], F32),
+    "AM0": ("sbuf", [128, 128], F32), "AM1": ("sbuf", [128, 128], F32),
+    "BM0": ("sbuf", [128, 128], F32), "BM1": ("sbuf", [128, 128], F32),
+    "Y0": ("sbuf", [128, 128], F32), "Y1": ("sbuf", [128, 128], F32),
+    "D0": ("sbuf", [128, 144], F32), "D1": ("sbuf", [128, 144], F32),
+    "R0": ("sbuf", [128, 144], F32), "R1": ("sbuf", [128, 144], F32),
+    "DE0": ("sbuf", [128, 128], F32), "DE1": ("sbuf", [128, 128], F32),
+    "YO16": ("sbuf", [128, 16], U16), "L3F": ("sbuf", [128, 16], F32),
+    "YU": ("sbuf", [128, 256], U16), "DEAD": ("sbuf", [128, 256], BF), "E": ("sbuf", [128, 4096], BF),
+    "CG": ("sbuf", [128, 256], F32), "SG": ("sbuf", [128, 256], F32),
+    "MM": ("sbuf", [128, 512], F32), "TT": ("sbuf", [128, 256], F32), "WW": ("sbuf", [128, 16], F32),
+    "DS": ("sbuf", [128, 256], F32), "RK": ("sbuf", [128, 256], BF), "DM": ("sbuf", [128, 16], F32),
+    "X": ("sbuf", [128, 32], F32), "X16": ("sbuf", [128, 32], U16),
+    "KR": ("sbuf", [128, 256], F32), "W1": ("sbuf", [128, 256], F32), "D2": ("sbuf", [128, 256], F32),
+    "KP0": ("psum", [128, 512], F32), "KP1": ("psum", [128, 512], F32), "ST": ("psum", [128, 512], F32),
+    "CON": ("psum", [128, 512], F32), "ROW": ("psum", [128, 512], F32), "DUP": ("psum", [128, 512], F32),
+    "CPB": ("psum", [128, 512], F32), "LP": ("psum", [128, 512], F32),
+}
+QUEUES = ("qv", "qs", "qt", "qp")
+DSEMS = ["dm%d" % i for i in range(12)]
+SEMAPHORES = list(QUEUES) + DSEMS + ["snd1", "snd2", "arr1", "arr2"]
+PSUM = {n for n in SCRATCH if SCRATCH[n][0] == "psum"}
+
+
+def rank_program(g, core, T, topo):
+    rank = T.rank_of(core)
+    if rank is None:
+        return
+    A, AF = AluOpType, ActivationFunctionType
+    eng = {"qv": g.vector, "qs": g.scalar, "qt": g.tensor, "qp": g, "sync": g.sync}
+    cnt, known, log, dmas = {}, {}, {}, [0]
+
+    def V(name, a=0, b=None, st=1, p=None):
+        n = SCRATCH[name][1][1]
+        b = n if b is None else b
+        t = T[name]
+        x = t[:, a:b:st] if p is None else t[p[0]:p[1], a:b:st]
+        return (x, name, a, b)
+
+    def need(q, w, r):
+        dep = {}
+        for views, wr in ((w, True), (r, False)):
+            for (_, name, a, b) in views:
+                ps = name in PSUM
+                for (lo, hi, ww, e, c) in log.get(name, ()):
+                    other = ps and e != q
+                    if not other and (hi <= a or b <= lo or not (wr or ww)):
+                        continue
+                    if ps and e == q == "qt":
+                        continue
+                    dep[e] = max(dep.get(e, 0), c)
+        for e in sorted(dep):
+            if known.get((q, e), 0) < dep[e]:
+                known[(q, e)] = dep[e]
+                eng[q].wait_ge(T.sem[e], dep[e])
+
+    def note(tok, w, r):
+        for views, wr in ((w, True), (r, False)):
+            for (_, name, a, b) in views:
+                ls = log.setdefault(name, [])
+                if wr:
+                    ls[:] = [x for x in ls if not (a <= x[0] and x[1] <= b)]
+                ls.append((a, b, wr, tok[0], tok[1]))
+
+    def op(q, fn, w, r):
+        need(q, w, r)
+        cnt[q] = cnt.get(q, 0) + 1
+        fn().then_inc(T.sem[q], 1)
+        note((q, cnt[q]), w, r)
+
+    def dma(q, out, in_, w, r):
+        need(q, w, r)
+        s = DSEMS[dmas[0]]
+        dmas[0] += 1
+        eng[q].dma_start(out, in_).then_inc(T.sem[s], 16)
+        note((s, 16), w, r)
+
+    def tt(out, a, b, o):
+        op("qv", lambda: g.vector.tensor_tensor(out[0], a[0], b[0], o), [out], [a, b])
+
+    def ts(out, a, s, o, s2=None, o2=None):
+        sc, rd = (s[0], [a, s]) if isinstance(s, tuple) else (s, [a])
+        if o2 is None:
+            op("qv", lambda: g.vector.tensor_scalar(out[0], a[0], sc, None, o), [out], rd)
+        else:
+            op("qv", lambda: g.vector.tensor_scalar(out[0], a[0], sc, s2, o, o2), [out], rd)
+
+    def cp(out, a):
+        op("qv", lambda: g.vector.tensor_copy(out[0], a[0]), [out], [a])
+
+    def scan(out, a, b, ini, o1, o2):
+        op("qv", lambda: g.vector.tensor_tensor_scan(out[0], a[0], b[0], ini, o1, o2), [out], [a, b])
+
+    def fill(out, c):
+        op("qv", lambda: g.vector.memset(out[0], c), [out], [])
+
+    def act(out, a, f=AF.Copy, **k):
+        rd = [a] + [x for x in k.values() if isinstance(x, tuple)]
+        kk = {n: (x[0] if isinstance(x, tuple) else x) for n, x in k.items()}
+        op("qs", lambda: g.scalar.activation(out[0], a[0], f, **kk), [out], rd)
+
+    def mm(out, l, r, start, stop):
+        op("qt", lambda: g.tensor.matmul(out[0], l[0], r[0], start, stop), [out], [l, r])
+
+    def iota(out, pat, base, cm):
+        op("qp", lambda: g.iota(out[0], pat, base, cm, allow_small_or_imprecise_dtypes=True), [out], [])
+
+    def asel(out, a, pat, o, base, cm):
+        op("qp", lambda: g.affine_select(out[0], a[0], pat, o, 0.0, base, cm), [out], [a])
+
+    dma("sync", T.SL[:, 1408:1984], T.s0[:, 1408:1984], [V("SL", 1408, 1984)], [])
+    dma("qs", T.CL[:, 992:1984], T.c0[:, 992:1984], [V("CL", 992, 1984)], [])
+    dma("sync", T.CL[:, 0:992], T.c0[:, 0:992], [V("CL", 0, 992)], [])
+    dma("sync", T.SL[:, 0:1408], T.s0[:, 0:1408], [V("SL", 0, 1408)], [])
+
+    fill(V("ONEB"), 1.0)
+    fill(V("ONEF"), 1.0)
+    fill(V("SW0"), 16.0)
+    iota(V("REPI"), [[1, 64]], 0, 0)
+    iota(V("PI"), [[1, 1]], 0, 1)
+    iota(V("IR"), [[0, 8], [1, 16]], 0, 0)
+    asel(V("BA"), V("ONEB"), [[-16, 8], [0, 16]], A.is_ge, 0, 1)
+    asel(V("BONES"), V("BA"), [[16, 8], [0, 16]], A.is_ge, 15, -1)
+    asel(V("SW1"), V("SW0"), [[-16, 8]], A.is_ge, 0, 1)
+    asel(V("SW16"), V("SW1"), [[16, 8]], A.is_ge, 15, -1)
+    asel(V("IDF"), V("ONEF"), [[-1, 128]], A.is_equal, 0, 1)
+    iota(V("SLOT"), [[16, 16]], COL - 128, 1)
+    iota(V("C", 128, 136), [[0, 8]], 0, 0)
+    iota(V("C", 2120, COL), [[0, 768]], 0, 0)
+    iota(V("S", 128, 136), [[0, 8]], 0, 0)
+    iota(V("S", 2120, COL), [[0, 768]], 0, 0)
+    cp(V("REPL"), V("REPI"))
+    ts(V("PA"), V("PI"), 15, A.bitwise_and)
+    cp(V("PM"), V("PA"))
+    ts(V("K8"), V("PM"), 0.03125, A.mult, 8.0, A.add)
+    ts(V("KB"), V("IR"), -1.0, A.mult, 15.0, A.add)
+    ts(V("PB"), V("IR"), 0.03125, A.mult, 8.0, A.add)
+    ZMP, SELP, M16P = V("CON", 0, 128), V("CON", 128, 256), V("CON", 256, 384)
+    ts(ZMP, V("IR"), 0.0, A.is_gt)
+    ts(SELP, V("IR"), 15.0, A.is_equal)
+    ts(M16P, V("IR"), V("PM"), A.is_equal)
+    ts(V("RST"), V("IR"), 0.0, A.is_gt, 33554432.0, A.mult)
+    ts(V("RST"), V("RST"), THR, A.max)
+    fill(V("Z3"), 1.0)
+    fill(V("Z3", 15, 144, 16), 0.0)
+    fill(V("D0", 128, 144), 0.0)
+    fill(V("D1", 128, 144), 0.0)
+    fill(V("ZERO"), 0.0)
+    ts(V("TC"), V("IR", 0, 16), V("PM"), A.is_gt)
+    ts(V("EQ"), V("IR", 0, 16), V("PM"), A.is_equal)
+
+    cp(V("S16E"), V("SL", 1408, 1984))
+    cp(V("S", PAD + 1408, PAD + 1984), V("SL", 1408, 1984))
+    cp(V("C", PAD + 992, PAD + 1984), V("CL", 992, 1984))
+    cp(V("C", PAD, PAD + 992), V("CL", 0, 992))
+
+    def more():
+        cp(V("S", PAD, PAD + 1408), V("SL", 0, 1408))
+        ts(V("DUMPY"), V("SLOT"), float(DSZ), A.add)
+        ts(V("Q0"), V("SW16"), 0.0625, A.mult)
+        cp(V("Q1", 0, 2), V("Q0", 6, 8))
+        cp(V("Q1", 2, 8), V("Q0", 0, 6))
+        cp(V("IDB"), V("IDF"))
+        cp(V("ID1", 0, 32), V("IDF", 96, 128))
+        cp(V("ID1", 32, 128), V("IDF", 0, 96))
+    late = [more]
+
+    def consts_on_scalar():
+        for c in range(1, 16):
+            act(V("TRI", 128 * c, 128 * c + 128), V("BONES"), scale=V("TC", c, c + 1))
+        for r in range(16):
+            act(V("SEL", 128 * r, 128 * r + 128), V("IDB"), scale=V("EQ", r, r + 1))
+
+    def argmax(b, n):
+        o, kp, st = 128 * b, V("KP%d" % b, 0, 128), V("ST", 128 * b, 128 * b + 128)
+        f, em, am, bm, y = (V(x + str(b)) for x in ("F", "EM", "AM", "BM", "Y"))
+        d, r, de = "D%d" % b, "R%d" % b, V("DE%d" % b)
+        scan(f, V("RST"), kp, THR, A.min, A.max)
+        tt(em, kp, f, A.is_equal)
+        tt(am, ZMP, em, A.is_gt)
+        tt(bm, em, st, A.mult)
+        scan(y, am, bm, 0.0, A.mult, A.add)
+        tt(V(d, 0, 128), y, SELP, A.mult)
+        scan(V(r, 0, 143), V("Z3", 0, 143), V(d, 0, 143), 0.0, A.mult, A.add)
+        tt(de, V(r, 15, 143), M16P, A.mult)
+        mm(V("LP", 8 * b, 8 * b + n // 16), de, V("Q%d" % b, 0, n // 16), True, True)
+        mm(V("ROW", o, o + n), V(r, 15, 143), V(("IDF", "ID1")[b], 0, n), True, True)
+
+    def step(u):
+        t, e = divmod(u, 2)
+        nb = 2 - e
+        L = (256 if t else 160) if e == 0 else 128
+        h, n0 = L // 16, 1984 + 128 * u
+        a = PAD + n0
+        ent = PAD + 1408 + 160 * t
+        ports = "P%d" % t
+        if e == 0:
+            xs = [(0, 160, ent)] + ([(160, 256, PAD + 1888)] if t else [])
+            cs = [(0, 160, "C", ent, "S16E", 160 * t)] + ([(160, 256, ports, 0, "S16E", 480)] if t else [])
+            blocks = [(0, 0, 128, 0), (128, 96, 32, 1)] + ([(160, 0, 96, 1)] if t else [])
+            chunks = [(0, 32), (32, 80), (80, 128), (128, 160)] + ([(160, 208), (208, 256)] if t else [])
+        else:
+            xs = [(0, 128, a - 128)]
+            cs = [(0, 128, "C", a - 128, "S16N", 0)]
+            blocks = [(0, 0, 128, 0)]
+            chunks = [(0, 16), (16, 48), (48, 88), (88, 128)]
+        top = PAD + (1984 if u == 0 else NV)
+        for b in range(nb):
+            for (po, m, c0) in [(0, 128, xs[0][2])] if b == 0 else [(96, 32, ent + 128), (0, 96, PAD + 1888)]:
+                out = V("ST", 128 * b, 128 * b + 128, p=(po, po + m))
+                mm(out, V("ONEF", 0, m, p=(0, 1)), V("PB", p=(0, 1)), True, False)
+                mm(out, V("S", c0, c0 + m), V("IDF"), False, True)
+        if u == 0:
+            mm(V("KP1", 0, 128, p=(0, 96)), V("ONEB", 0, 96, p=(0, 1)), V("KB", p=(0, 1)), True, True)
+        for (l0, l1) in chunks:
+            lo, hi, cb, cc, sb, so = [x for x in cs if x[0] <= l0 < x[1]][0]
+            src = V(cb, cc + l0 - lo, cc + l1 - lo)
+            rep, off = V("REPL", 0, l1 - l0), V(sb, so + l0 - lo, so + l1 - lo)
+            cx, mn = V("CX", 16 * l0, 16 * l1), V("MN", 16 * l0, 16 * l1)
+            op("qs", lambda: g.scalar.activation(cx[0], src[0].indirect(rep[0]), AF.Copy), [cx], [src, rep])
+            win = V("C", PAD, top)
+            op("qv", lambda: g.vector.tensor_tensor(mn[0], win[0].indirect(off[0]), cx[0], A.min), [mn], [win, off, cx])
+            for (bl, po, m, b) in blocks:
+                if bl + m == l1:
+                    mm(V("KP%d" % b, 0, 128, p=(po, po + m)), V("ONEB", 0, m, p=(0, 1)), V("KB", p=(0, 1)), True, False)
+                    for k in range(16):
+                        mm(V("KP%d" % b, k, 128, 16, p=(po, po + m)), V("MN", 16 * bl + k, 16 * (bl + m - 1) + k + 1, 16),
+                           V("SW16"), False, k == 15)
+        for f in late:
+            f()
+        late.clear()
+        if u == 0:
+            consts_on_scalar()
+        for (lo, hi, cb, cc, sb, so) in cs:
+            act(V("CPB", lo, hi), V(cb, cc, cc + hi - lo))
+        for b in range(nb):
+            argmax(b, min(128, L - 128 * b))
+        lp, yo, l3 = V("LP", 0, h), V("YO16", 0, h), V("L3F", 0, h)
+        cp(yo, lp)
+        cp(V("YU", 0, L), V("ROW", 0, L))
+        cp(l3, yo)
+        cg, sg = V("CG", 0, L), V("SG", 0, L)
+        cwin, swin = V("C", 128, COL), V("S", 128, COL)
+        op("qs", lambda: g.scalar.activation(cg[0], cwin[0].indirect(yo[0]), AF.Copy), [cg], [cwin, yo])
+        op("qs", lambda: g.scalar.activation(sg[0], swin[0].indirect(yo[0]), AF.Copy), [sg], [swin, yo])
+        ts(V("DEAD", 0, L), V("YU", 0, L), 0.0, A.is_equal)
+        mm(V("DUP", 0, L), V("BONES"), V("DEAD", 0, L), True, False)
+        for q in range(h):
+            ts(V("E", 256 * q, 256 * q + L - 16 * q), V("YU", 16 * q, L), V("L3F", q, q + 1), A.is_equal)
+            if q < h - 1:
+                mm(V("DUP", 16 * q + 16, L), V("BONES"), V("E", 256 * q + 16, 256 * q + L - 16 * q), False, False)
+        for c in range(1, 16):
+            mm(V("DUP", c, L, 16), V("TRI", 128 * c, 128 * c + 128), V("E", c, 256 * (h - 1) + c + 1, 256), False, c == 15)
+        m, c_, tmp = V("MM", 0, L), V("CPB", 0, L), V("TT", 0, L)
+        tt(m, cg, c_, A.min)
+        tt(tmp, cg, c_, A.subtract)
+        act(V("MM", 256, 256 + L), tmp, AF.Relu)
+        w = V("WW", 0, h)
+        tt(w, V("DUMPY", 0, h), l3, A.subtract)
+        ts(V("DUMPN", 0, h), V("SLOT", 0, h), float(-a), A.add)
+        stn, ds, rk = V("CPB", 256, 256 + L), V("DS", 0, L), V("RK", 0, L)
+        ts(stn, V("DUP", 0, L), 0.0, A.is_equal, -1.0, A.mult)
+        scan(ds, stn, V("ZERO", 0, L), 129.0, A.add, A.max)
+        tt(rk, ds, stn, A.mult)
+        rp = V("LP", 16, 16 + h)
+        for r in range(16):
+            mm(rp, V("SEL", 128 * r, 128 * r + 128), V("RK", r, L, 16), r == 0, r == 15)
+        dm = V("DM", 0, h)
+        xn, xy = V("X", 0, h), V("X", h, 2 * h)
+        ts(dm, rp, 0.0, A.is_equal)
+        tt(xn, dm, V("DUMPN", 0, h), A.mult)
+        tt(xy, dm, w, A.mult)
+        tt(xn, xn, rp, A.add)
+        tt(xy, xy, l3, A.add)
+        ts(V("X16", 0, 2 * h), V("X", 0, 2 * h), 128.0, A.add)
+        on, oy = V("X16", 0, h), V("X16", h, 2 * h)
+
+        def scatter(win, off, src):
+            op("qv", lambda: g.vector.tensor_copy(win[0].indirect(off[0]), src[0]), [win], [off, src])
+        scatter(V("S", a, SW), on, sg)
+        scatter(V("C", a, CW), on, m)
+        scatter(V("C", 0, CW), oy, V("MM", 256, 256 + L))
+        if e == 0:
+            cp(V("S16N"), V("S", a, a + 128))
+
+        def links():
+            kr, nr = V("KR", 0, L), V("CPB", 256, 256 + L)
+            mk = V("DUP", 256, 256 + L)
+            act(kr, rk, AF.Sign, scale=-1.0)
+            act(nr, rk, AF.Copy, bias=float(n0 + 128))
+            for (lo, hi, c) in xs:
+                tt(V("W1", lo, hi), V("ROW", lo, hi), V("S", c, c + hi - lo), A.subtract)
+            ts(mk, V("W1", 0, L), V("K8"), A.is_equal)
+            for (lo, hi, c) in xs:
+                tt(V("D2", lo, hi), V("CPB", 256 + lo, 256 + hi), V("S", c, c + hi - lo), A.subtract)
+            tt(mk, kr, mk, A.mult)
+            tt(mk, V("D2", 0, L), mk, A.mult)
+            for (lo, hi, c) in xs:
+                x = V("S", c, c + hi - lo)
+                tt(x, x, V("DUP", 256 + lo, 256 + hi), A.add)
+            if u == 2:
+                cp(V("S16E", 480, 576), V("S", PAD + 1888, PAD + 1984))
+            if u == 4:
+                dma("sync", T.ys[:, 0:1088], T.S[:, PAD + 1408:PAD + 2496], [], [V("S", PAD + 1408, PAD + 2496)])
+        late.append(links)
+
+        if e == 1 and t < 2:
+            nxt, prv = T.cores[(rank + 1) % len(T.cores)], T.cores[(rank - 1) % len(T.cores)]
+            rid, pid = topo.addr(nxt)[:2]
+            me, got = topo.engines(core, nxt)[:8], len(topo.engines(prv, core)[:8])
+            src, dst = V("C", a, a + 96), V("P%d" % (t + 1))
+            snd, arr = "snd%d" % (t + 1), "arr%d" % (t + 1)
+            need("qp", [], [src])
+            g.remote_dma(dst[0], src[0], T.sem[arr], T.sem[snd], pid, rid, sum(1 << i for i in me))
+            note((snd, len(me)), [], [src])
+            note((arr, got), [dst], [])
+
+    for u in range(6):
+        step(u)
+    dma("sync", T.yc[:, :], T.C[:, PAD:COL], [], [V("C", PAD, COL)])
+    late[0]()
+    dma("sync", T.ys[:, 1088:1344], T.S[:, PAD + 2496:COL], [], [V("S", PAD + 2496, COL)])
+    for s in range(dmas[0]):
+        g.sync.wait_ge(T.sem[DSEMS[s]], 16)
+    for q in QUEUES:
+        g.sync.wait_ge(T.sem[q], cnt[q])

@@ -17,32 +17,28 @@ SCRATCH = {
     "CX": ("sbuf", [128, 4096], F32), "MN": ("sbuf", [128, 4096], F32),
     "REPI": ("sbuf", [128, 64], I32), "REPL": ("sbuf", [128, 64], U16),
     "PI": ("sbuf", [128, 1], I32), "PA": ("sbuf", [128, 1], I32), "PM": ("sbuf", [128, 1], F32),
-    "K8": ("sbuf", [128, 1], F32), "IR": ("sbuf", [128, 128], F32),
+    "IR": ("sbuf", [128, 128], F32),
     "ONEF": ("sbuf", [128, 128], F32), "ONEB": ("sbuf", [128, 128], BF),
-    "IDF": ("sbuf", [128, 128], F32), "ID1": ("sbuf", [128, 128], F32), "IDB": ("sbuf", [128, 128], BF),
+    "IDF": ("sbuf", [128, 128], F32), "ID1": ("sbuf", [128, 128], F32),
+    "IDB": ("sbuf", [128, 128], BF), "IB1": ("sbuf", [128, 128], BF),
     "BA": ("sbuf", [128, 128], BF), "BONES": ("sbuf", [128, 128], BF),
     "TC": ("sbuf", [128, 16], F32), "EQ": ("sbuf", [128, 16], F32),
     "TRI": ("sbuf", [128, 2048], BF), "SEL": ("sbuf", [128, 2048], BF),
     "SW0": ("sbuf", [128, 8], F32), "SW1": ("sbuf", [128, 8], F32), "SW16": ("sbuf", [128, 8], F32),
     "Q0": ("sbuf", [128, 8], F32), "Q1": ("sbuf", [128, 8], F32),
     "KB": ("sbuf", [128, 128], BF), "PB": ("sbuf", [128, 128], F32), "RST": ("sbuf", [128, 128], F32),
-    "Z3": ("sbuf", [128, 144], F32), "ZERO": ("sbuf", [128, 256], F32),
-    "SLOT": ("sbuf", [128, 16], F32), "DUMPY": ("sbuf", [128, 16], F32), "DUMPN": ("sbuf", [128, 16], F32),
-    "F0": ("sbuf", [128, 128], F32), "F1": ("sbuf", [128, 128], F32),
-    "EM0": ("sbuf", [128, 128], F32), "EM1": ("sbuf", [128, 128], F32),
-    "AM0": ("sbuf", [128, 128], F32), "AM1": ("sbuf", [128, 128], F32),
-    "BM0": ("sbuf", [128, 128], F32), "BM1": ("sbuf", [128, 128], F32),
-    "Y0": ("sbuf", [128, 128], F32), "Y1": ("sbuf", [128, 128], F32),
-    "D0": ("sbuf", [128, 144], F32), "D1": ("sbuf", [128, 144], F32),
-    "R0": ("sbuf", [128, 144], F32), "R1": ("sbuf", [128, 144], F32),
-    "DE0": ("sbuf", [128, 128], F32), "DE1": ("sbuf", [128, 128], F32),
+    "Z3": ("sbuf", [128, 143], F32), "ZERO": ("sbuf", [128, 256], F32),
+    "DUMPY": ("sbuf", [128, 16], F32), "DUMPN": ("sbuf", [128, 96], F32),
+    "F": ("sbuf", [128, 256], F32), "EM": ("sbuf", [128, 256], F32), "AM": ("sbuf", [128, 256], F32),
+    "BM": ("sbuf", [128, 256], F32), "Y": ("sbuf", [128, 256], F32), "DE": ("sbuf", [128, 256], F32),
+    "D": ("sbuf", [128, 288], F32), "R": ("sbuf", [128, 288], F32), "WB": ("sbuf", [128, 256], BF),
     "YO16": ("sbuf", [128, 16], U16), "L3F": ("sbuf", [128, 16], F32),
-    "YU": ("sbuf", [128, 256], U16), "DEAD": ("sbuf", [128, 256], BF), "E": ("sbuf", [128, 4096], BF),
+    "YU": ("sbuf", [128, 256], U16), "LV": ("sbuf", [128, 256], BF), "E": ("sbuf", [128, 4096], BF),
     "CG": ("sbuf", [128, 256], F32), "SG": ("sbuf", [128, 256], F32),
-    "MM": ("sbuf", [128, 512], F32), "TT": ("sbuf", [128, 256], F32), "WW": ("sbuf", [128, 16], F32),
+    "MM": ("sbuf", [128, 256], F32), "WW": ("sbuf", [128, 16], F32),
     "DS": ("sbuf", [128, 256], F32), "RK": ("sbuf", [128, 256], BF), "DM": ("sbuf", [128, 16], F32),
     "X": ("sbuf", [128, 32], F32), "X16": ("sbuf", [128, 32], U16),
-    "KR": ("sbuf", [128, 256], F32), "W1": ("sbuf", [128, 256], F32), "D2": ("sbuf", [128, 256], F32),
+    "KR": ("sbuf", [128, 256], F32), "NK": ("sbuf", [128, 256], F32),
     "KP0": ("psum", [128, 512], F32), "KP1": ("psum", [128, 512], F32), "ST": ("psum", [128, 512], F32),
     "CON": ("psum", [128, 512], F32), "ROW": ("psum", [128, 512], F32), "DUP": ("psum", [128, 512], F32),
     "CPB": ("psum", [128, 512], F32), "LP": ("psum", [128, 512], F32),
@@ -140,8 +136,9 @@ def rank_program(g, core, T, topo):
         op("qp", lambda: g.affine_select(out[0], a[0], pat, o, 0.0, base, cm), [out], [a])
 
     dma("sync", T.SL[:, 1408:1984], T.s0[:, 1408:1984], [V("SL", 1408, 1984)], [])
-    dma("qs", T.CL[:, 992:1984], T.c0[:, 992:1984], [V("CL", 992, 1984)], [])
-    dma("sync", T.CL[:, 0:992], T.c0[:, 0:992], [V("CL", 0, 992)], [])
+    dma("qs", T.CL[:, 1408:1984], T.c0[:, 1408:1984], [V("CL", 1408, 1984)], [])
+    dma("sync", T.CL[:, 0:704], T.c0[:, 0:704], [V("CL", 0, 704)], [])
+    dma("qs", T.CL[:, 704:1408], T.c0[:, 704:1408], [V("CL", 704, 1408)], [])
     dma("sync", T.SL[:, 0:1408], T.s0[:, 0:1408], [V("SL", 0, 1408)], [])
 
     fill(V("ONEB"), 1.0)
@@ -155,15 +152,16 @@ def rank_program(g, core, T, topo):
     asel(V("SW1"), V("SW0"), [[-16, 8]], A.is_ge, 0, 1)
     asel(V("SW16"), V("SW1"), [[16, 8]], A.is_ge, 15, -1)
     asel(V("IDF"), V("ONEF"), [[-1, 128]], A.is_equal, 0, 1)
-    iota(V("SLOT"), [[16, 16]], COL - 128, 1)
     iota(V("C", 128, 136), [[0, 8]], 0, 0)
     iota(V("C", 2120, COL), [[0, 768]], 0, 0)
     iota(V("S", 128, 136), [[0, 8]], 0, 0)
     iota(V("S", 2120, COL), [[0, 768]], 0, 0)
+    iota(V("DUMPY"), [[16, 16]], COL + DSZ - 128, 1)
+    for u in range(6):
+        iota(V("DUMPN", 16 * u, 16 * u + 16), [[16, 16]], COL - 128 - (PAD + 1984 + 128 * u), 1)
     cp(V("REPL"), V("REPI"))
     ts(V("PA"), V("PI"), 15, A.bitwise_and)
     cp(V("PM"), V("PA"))
-    ts(V("K8"), V("PM"), 0.03125, A.mult, 8.0, A.add)
     ts(V("KB"), V("IR"), -1.0, A.mult, 15.0, A.add)
     ts(V("PB"), V("IR"), 0.03125, A.mult, 8.0, A.add)
     ZMP, SELP, M16P = V("CON", 0, 128), V("CON", 128, 256), V("CON", 256, 384)
@@ -173,49 +171,51 @@ def rank_program(g, core, T, topo):
     ts(V("RST"), V("IR"), 0.0, A.is_gt, 33554432.0, A.mult)
     ts(V("RST"), V("RST"), THR, A.max)
     fill(V("Z3"), 1.0)
-    fill(V("Z3", 15, 144, 16), 0.0)
-    fill(V("D0", 128, 144), 0.0)
-    fill(V("D1", 128, 144), 0.0)
+    fill(V("Z3", 15, 143, 16), 0.0)
+    fill(V("D", 128, 144), 0.0)
+    fill(V("D", 272, 288), 0.0)
     fill(V("ZERO"), 0.0)
     ts(V("TC"), V("IR", 0, 16), V("PM"), A.is_gt)
     ts(V("EQ"), V("IR", 0, 16), V("PM"), A.is_equal)
 
     cp(V("S16E"), V("SL", 1408, 1984))
+    cp(V("C", PAD + 1408, PAD + 1568), V("CL", 1408, 1568))
     cp(V("S", PAD + 1408, PAD + 1984), V("SL", 1408, 1984))
-    cp(V("C", PAD + 992, PAD + 1984), V("CL", 992, 1984))
-    cp(V("C", PAD, PAD + 992), V("CL", 0, 992))
+    cp(V("C", PAD + 1568, PAD + 1984), V("CL", 1568, 1984))
+    cp(V("C", PAD, PAD + 704), V("CL", 0, 704))
 
     def more():
+        cp(V("C", PAD + 704, PAD + 1408), V("CL", 704, 1408))
         cp(V("S", PAD, PAD + 1408), V("SL", 0, 1408))
-        ts(V("DUMPY"), V("SLOT"), float(DSZ), A.add)
-        ts(V("Q0"), V("SW16"), 0.0625, A.mult)
-        cp(V("Q1", 0, 2), V("Q0", 6, 8))
-        cp(V("Q1", 2, 8), V("Q0", 0, 6))
-        cp(V("IDB"), V("IDF"))
-        cp(V("ID1", 0, 32), V("IDF", 96, 128))
-        cp(V("ID1", 32, 128), V("IDF", 0, 96))
     late = [more]
 
     def consts_on_scalar():
+        act(V("Q0"), V("SW16"), scale=0.0625)
+        act(V("Q1", 0, 2), V("Q0", 6, 8))
+        act(V("Q1", 2, 8), V("Q0", 0, 6))
+        act(V("ID1", 0, 32), V("IDF", 96, 128))
+        act(V("ID1", 32, 128), V("IDF", 0, 96))
+        act(V("IDB"), V("IDF"))
+        act(V("IB1"), V("ID1"))
         for c in range(1, 16):
             act(V("TRI", 128 * c, 128 * c + 128), V("BONES"), scale=V("TC", c, c + 1))
         for r in range(16):
             act(V("SEL", 128 * r, 128 * r + 128), V("IDB"), scale=V("EQ", r, r + 1))
 
-    def argmax(b, n):
-        o, kp, st = 128 * b, V("KP%d" % b, 0, 128), V("ST", 128 * b, 128 * b + 128)
-        f, em, am, bm, y = (V(x + str(b)) for x in ("F", "EM", "AM", "BM", "Y"))
-        d, r, de = "D%d" % b, "R%d" % b, V("DE%d" % b)
+    def argmax(b, w):
+        o, kp = 128 * b, V("KP%d" % b, 0, 128)
+        o1, q = o + 128, 144 * b
+        f, em, am, bm, y, st, de = (V(x, o, o1) for x in ("F", "EM", "AM", "BM", "Y", "ST", "DE"))
         scan(f, V("RST"), kp, THR, A.min, A.max)
         tt(em, kp, f, A.is_equal)
         tt(am, ZMP, em, A.is_gt)
         tt(bm, em, st, A.mult)
         scan(y, am, bm, 0.0, A.mult, A.add)
-        tt(V(d, 0, 128), y, SELP, A.mult)
-        scan(V(r, 0, 143), V("Z3", 0, 143), V(d, 0, 143), 0.0, A.mult, A.add)
-        tt(de, V(r, 15, 143), M16P, A.mult)
-        mm(V("LP", 8 * b, 8 * b + n // 16), de, V("Q%d" % b, 0, n // 16), True, True)
-        mm(V("ROW", o, o + n), V(r, 15, 143), V(("IDF", "ID1")[b], 0, n), True, True)
+        tt(V("D", q, q + 128), y, SELP, A.mult)
+        scan(V("R", q, q + 143), V("Z3"), V("D", q, q + 143), 0.0, A.mult, A.add)
+        tt(de, V("R", q + 15, q + 143), M16P, A.mult)
+        mm(V("LP", 8 * b, 8 * b + w // 16), de, V("Q%d" % b, 0, w // 16), True, True)
+        mm(V("ROW", o, o + w), V("R", q + 15, q + 143), V(("IDF", "ID1")[b], 0, w), True, True)
 
     def step(u):
         t, e = divmod(u, 2)
@@ -229,13 +229,12 @@ def rank_program(g, core, T, topo):
             xs = [(0, 160, ent)] + ([(160, 256, PAD + 1888)] if t else [])
             cs = [(0, 160, "C", ent, "S16E", 160 * t)] + ([(160, 256, ports, 0, "S16E", 480)] if t else [])
             blocks = [(0, 0, 128, 0), (128, 96, 32, 1)] + ([(160, 0, 96, 1)] if t else [])
-            chunks = [(0, 32), (32, 80), (80, 128), (128, 160)] + ([(160, 208), (208, 256)] if t else [])
+            chunks = [(0, 16), (16, 48), (48, 88), (88, 128), (128, 160)] + ([(160, 208), (208, 256)] if t else [])
         else:
             xs = [(0, 128, a - 128)]
             cs = [(0, 128, "C", a - 128, "S16N", 0)]
             blocks = [(0, 0, 128, 0)]
-            chunks = [(0, 16), (16, 48), (48, 88), (88, 128)]
-        top = PAD + (1984 if u == 0 else NV)
+            chunks = [(0, 32), (32, 64), (64, 96), (96, 128)]
         for b in range(nb):
             for (po, m, c0) in [(0, 128, xs[0][2])] if b == 0 else [(96, 32, ent + 128), (0, 96, PAD + 1888)]:
                 out = V("ST", 128 * b, 128 * b + 128, p=(po, po + m))
@@ -249,7 +248,7 @@ def rank_program(g, core, T, topo):
             rep, off = V("REPL", 0, l1 - l0), V(sb, so + l0 - lo, so + l1 - lo)
             cx, mn = V("CX", 16 * l0, 16 * l1), V("MN", 16 * l0, 16 * l1)
             op("qs", lambda: g.scalar.activation(cx[0], src[0].indirect(rep[0]), AF.Copy), [cx], [src, rep])
-            win = V("C", PAD, top)
+            win = V("CL") if u == 0 else V("C", PAD, COL)
             op("qv", lambda: g.vector.tensor_tensor(mn[0], win[0].indirect(off[0]), cx[0], A.min), [mn], [win, off, cx])
             for (bl, po, m, b) in blocks:
                 if bl + m == l1:
@@ -270,65 +269,60 @@ def rank_program(g, core, T, topo):
         cp(yo, lp)
         cp(V("YU", 0, L), V("ROW", 0, L))
         cp(l3, yo)
+        lv = V("LV", 0, L)
+        act(lv, V("ROW", 0, L), AF.Sign, scale=-1.0)
         cg, sg = V("CG", 0, L), V("SG", 0, L)
         cwin, swin = V("C", 128, COL), V("S", 128, COL)
         op("qs", lambda: g.scalar.activation(cg[0], cwin[0].indirect(yo[0]), AF.Copy), [cg], [cwin, yo])
         op("qs", lambda: g.scalar.activation(sg[0], swin[0].indirect(yo[0]), AF.Copy), [sg], [swin, yo])
-        ts(V("DEAD", 0, L), V("YU", 0, L), 0.0, A.is_equal)
-        mm(V("DUP", 0, L), V("BONES"), V("DEAD", 0, L), True, False)
+        mm(V("DUP", 0, L), V("BONES"), lv, True, False)
         for q in range(h):
             ts(V("E", 256 * q, 256 * q + L - 16 * q), V("YU", 16 * q, L), V("L3F", q, q + 1), A.is_equal)
             if q < h - 1:
                 mm(V("DUP", 16 * q + 16, L), V("BONES"), V("E", 256 * q + 16, 256 * q + L - 16 * q), False, False)
         for c in range(1, 16):
             mm(V("DUP", c, L, 16), V("TRI", 128 * c, 128 * c + 128), V("E", c, 256 * (h - 1) + c + 1, 256), False, c == 15)
-        m, c_, tmp = V("MM", 0, L), V("CPB", 0, L), V("TT", 0, L)
-        tt(m, cg, c_, A.min)
-        tt(tmp, cg, c_, A.subtract)
-        act(V("MM", 256, 256 + L), tmp, AF.Relu)
-        w = V("WW", 0, h)
-        tt(w, V("DUMPY", 0, h), l3, A.subtract)
-        ts(V("DUMPN", 0, h), V("SLOT", 0, h), float(-a), A.add)
+        for b in range(nb):
+            tt(V("WB", 128 * b, 128 * b + 128), V("ST", 128 * b, 128 * b + 128), V("R", 144 * b + 15, 144 * b + 143), A.is_equal)
+        m = V("MM", 0, L)
+        tt(m, cg, V("CPB", 0, L), A.min)
         stn, ds, rk = V("CPB", 256, 256 + L), V("DS", 0, L), V("RK", 0, L)
-        ts(stn, V("DUP", 0, L), 0.0, A.is_equal, -1.0, A.mult)
+        ts(stn, V("DUP", 0, L), -16.0, A.is_equal, -1.0, A.mult)
         scan(ds, stn, V("ZERO", 0, L), 129.0, A.add, A.max)
         tt(rk, ds, stn, A.mult)
         rp = V("LP", 16, 16 + h)
         for r in range(16):
             mm(rp, V("SEL", 128 * r, 128 * r + 128), V("RK", r, L, 16), r == 0, r == 15)
+        for b, x in enumerate((128,) if e else (128, L - 128)):
+            mm(V("ROW", 256 + 128 * b, 256 + 128 * b + x), V("WB", 128 * b, 128 * b + 128), V(("IDB", "IB1")[b], 0, x), True, True)
+        kr, kn = V("KR", 0, L), V("CPB", 256, 256 + L)
+        act(kr, rk, AF.Sign, scale=-1.0)
+        act(kn, kr, AF.Copy, scale=float(n0 + 128))
+        w = V("WW", 0, h)
+        tt(w, V("DUMPY", 0, h), l3, A.subtract)
         dm = V("DM", 0, h)
         xn, xy = V("X", 0, h), V("X", h, 2 * h)
         ts(dm, rp, 0.0, A.is_equal)
-        tt(xn, dm, V("DUMPN", 0, h), A.mult)
+        tt(xn, dm, V("DUMPN", 16 * u, 16 * u + h), A.mult)
         tt(xy, dm, w, A.mult)
         tt(xn, xn, rp, A.add)
         tt(xy, xy, l3, A.add)
         ts(V("X16", 0, 2 * h), V("X", 0, 2 * h), 128.0, A.add)
         on, oy = V("X16", 0, h), V("X16", h, 2 * h)
-
-        def scatter(win, off, src):
-            op("qv", lambda: g.vector.tensor_copy(win[0].indirect(off[0]), src[0]), [win], [off, src])
-        scatter(V("S", a, SW), on, sg)
-        scatter(V("C", a, CW), on, m)
-        scatter(V("C", 0, CW), oy, V("MM", 256, 256 + L))
+        op("qv", lambda: g.vector.tensor_copy(T.C[:, a:CW].indirect(on[0]), m[0]), [V("C", a, CW)], [on, m])
+        op("qv", lambda: g.vector.tensor_tensor(T.C[:].indirect(oy[0]), cg[0], m[0], A.subtract), [V("C")], [oy, cg, m])
+        if u == 5:
+            dma("sync", T.yc[:, :], T.C[:, PAD:COL], [], [V("C", PAD, COL)])
+        op("qv", lambda: g.vector.tensor_copy(T.S[:, a:SW].indirect(on[0]), sg[0]), [V("S", a, SW)], [on, sg])
         if e == 0:
             cp(V("S16N"), V("S", a, a + 128))
 
         def links():
-            kr, nr = V("KR", 0, L), V("CPB", 256, 256 + L)
-            mk = V("DUP", 256, 256 + L)
-            act(kr, rk, AF.Sign, scale=-1.0)
-            act(nr, rk, AF.Copy, bias=float(n0 + 128))
-            for (lo, hi, c) in xs:
-                tt(V("W1", lo, hi), V("ROW", lo, hi), V("S", c, c + hi - lo), A.subtract)
-            ts(mk, V("W1", 0, L), V("K8"), A.is_equal)
-            for (lo, hi, c) in xs:
-                tt(V("D2", lo, hi), V("CPB", 256 + lo, 256 + hi), V("S", c, c + hi - lo), A.subtract)
-            tt(mk, kr, mk, A.mult)
-            tt(mk, V("D2", 0, L), mk, A.mult)
+            tt(V("NK", 0, L), kn, rk, A.add)
+            tt(kn, V("NK", 0, L), V("ROW", 256, 256 + L), A.mult)
             for (lo, hi, c) in xs:
                 x = V("S", c, c + hi - lo)
-                tt(x, x, V("DUP", 256 + lo, 256 + hi), A.add)
+                tt(x, x, V("CPB", 256 + lo, 256 + hi), A.max)
             if u == 2:
                 cp(V("S16E", 480, 576), V("S", PAD + 1888, PAD + 1984))
             if u == 4:
@@ -348,7 +342,6 @@ def rank_program(g, core, T, topo):
 
     for u in range(6):
         step(u)
-    dma("sync", T.yc[:, :], T.C[:, PAD:COL], [], [V("C", PAD, COL)])
     late[0]()
     dma("sync", T.ys[:, 1088:1344], T.S[:, PAD + 2496:COL], [], [V("S", PAD + 2496, COL)])
     for s in range(dmas[0]):

@@ -26,13 +26,13 @@ SCRATCH = {
     "TRI": ("sbuf", [128, 2048], BF), "SEL": ("sbuf", [128, 2048], BF),
     "SW0": ("sbuf", [128, 8], F32), "SW1": ("sbuf", [128, 8], F32), "SW16": ("sbuf", [128, 8], F32),
     "Q0": ("sbuf", [128, 8], F32), "Q1": ("sbuf", [128, 8], F32),
-    "KB": ("sbuf", [128, 128], BF), "PB": ("sbuf", [128, 128], F32), "RST": ("sbuf", [128, 128], F32),
-    "Z3": ("sbuf", [128, 143], F32), "ZERO": ("sbuf", [128, 256], F32),
+    "KB": ("sbuf", [128, 128], BF), "PB": ("sbuf", [128, 128], BF), "RST": ("sbuf", [128, 128], F32),
+    "Z3": ("sbuf", [128, 272], F32), "ZERO": ("sbuf", [128, 256], F32),
     "DUMPY": ("sbuf", [128, 16], F32), "DUMPN": ("sbuf", [128, 96], F32),
     "F": ("sbuf", [128, 256], F32), "EM": ("sbuf", [128, 256], F32), "AM": ("sbuf", [128, 256], F32),
-    "BM": ("sbuf", [128, 256], F32), "Y": ("sbuf", [128, 256], F32), "DE": ("sbuf", [128, 256], F32),
-    "D": ("sbuf", [128, 288], F32), "R": ("sbuf", [128, 288], F32), "WB": ("sbuf", [128, 256], BF),
-    "YO16": ("sbuf", [128, 16], U16), "L3F": ("sbuf", [128, 16], F32),
+    "Y": ("sbuf", [128, 256], F32), "DE": ("sbuf", [128, 256], F32),
+    "D": ("sbuf", [128, 272], F32), "R": ("sbuf", [128, 272], F32), "WB": ("sbuf", [128, 256], BF),
+    "YO16": ("sbuf", [128, 16], U16),
     "YU": ("sbuf", [128, 256], U16), "LV": ("sbuf", [128, 256], BF), "E": ("sbuf", [128, 4096], BF),
     "CG": ("sbuf", [128, 256], F32), "SG": ("sbuf", [128, 256], F32),
     "MM": ("sbuf", [128, 256], F32), "WW": ("sbuf", [128, 16], F32),
@@ -135,10 +135,21 @@ def rank_program(g, core, T, topo):
     def asel(out, a, pat, o, base, cm):
         op("qp", lambda: g.affine_select(out[0], a[0], pat, o, 0.0, base, cm), [out], [a])
 
-    dma("sync", T.SL[:, 1408:1984], T.s0[:, 1408:1984], [V("SL", 1408, 1984)], [])
+    def mix(*chains):
+        chains = [iter(c) for c in chains]
+        while chains:
+            for c in list(chains):
+                f = next(c, None)
+                if f is None:
+                    chains.remove(c)
+                else:
+                    f()
+
+    dma("sync", T.SL[:, 1408:1568], T.s0[:, 1408:1568], [V("SL", 1408, 1568)], [])
     dma("qs", T.CL[:, 1408:1984], T.c0[:, 1408:1984], [V("CL", 1408, 1984)], [])
     dma("sync", T.CL[:, 0:704], T.c0[:, 0:704], [V("CL", 0, 704)], [])
     dma("qs", T.CL[:, 704:1408], T.c0[:, 704:1408], [V("CL", 704, 1408)], [])
+    dma("sync", T.SL[:, 1568:1984], T.s0[:, 1568:1984], [V("SL", 1568, 1984)], [])
     dma("sync", T.SL[:, 0:1408], T.s0[:, 0:1408], [V("SL", 0, 1408)], [])
 
     fill(V("ONEB"), 1.0)
@@ -163,30 +174,31 @@ def rank_program(g, core, T, topo):
     ts(V("PA"), V("PI"), 15, A.bitwise_and)
     cp(V("PM"), V("PA"))
     ts(V("KB"), V("IR"), -1.0, A.mult, 15.0, A.add)
-    ts(V("PB"), V("IR"), 0.03125, A.mult, 8.0, A.add)
-    ZMP, SELP, M16P = V("CON", 0, 128), V("CON", 128, 256), V("CON", 256, 384)
+    fill(V("PB"), 8.0)
+    ZMP = V("CON", 0, 128)
     ts(ZMP, V("IR"), 0.0, A.is_gt)
-    ts(SELP, V("IR"), 15.0, A.is_equal)
-    ts(M16P, V("IR"), V("PM"), A.is_equal)
+    ts(V("CON", 128, 256), V("IR"), V("PM"), A.is_equal)
+    ts(V("CON", 256, 384), V("IR"), V("PM"), A.is_equal)
     ts(V("RST"), V("IR"), 0.0, A.is_gt, 33554432.0, A.mult)
     ts(V("RST"), V("RST"), THR, A.max)
     fill(V("Z3"), 1.0)
-    fill(V("Z3", 15, 143, 16), 0.0)
-    fill(V("D", 128, 144), 0.0)
-    fill(V("D", 272, 288), 0.0)
+    fill(V("Z3", 15, 272, 16), 0.0)
+    fill(V("D"), 0.0)
     fill(V("ZERO"), 0.0)
     ts(V("TC"), V("IR", 0, 16), V("PM"), A.is_gt)
     ts(V("EQ"), V("IR", 0, 16), V("PM"), A.is_equal)
 
-    cp(V("S16E"), V("SL", 1408, 1984))
+    cp(V("S16E", 0, 160), V("SL", 1408, 1568))
     cp(V("C", PAD + 1408, PAD + 1568), V("CL", 1408, 1568))
-    cp(V("S", PAD + 1408, PAD + 1984), V("SL", 1408, 1984))
+    cp(V("S", PAD + 1408, PAD + 1568), V("SL", 1408, 1568))
     cp(V("C", PAD + 1568, PAD + 1984), V("CL", 1568, 1984))
     cp(V("C", PAD, PAD + 704), V("CL", 0, 704))
 
     def more():
-        cp(V("C", PAD + 704, PAD + 1408), V("CL", 704, 1408))
-        cp(V("S", PAD, PAD + 1408), V("SL", 0, 1408))
+        yield lambda: cp(V("C", PAD + 704, PAD + 1408), V("CL", 704, 1408))
+        yield lambda: cp(V("S16E", 160, 576), V("SL", 1568, 1984))
+        yield lambda: cp(V("S", PAD + 1568, PAD + 1984), V("SL", 1568, 1984))
+        yield lambda: cp(V("S", PAD, PAD + 1408), V("SL", 0, 1408))
     late = [more]
 
     def consts_on_scalar():
@@ -202,20 +214,26 @@ def rank_program(g, core, T, topo):
         for r in range(16):
             act(V("SEL", 128 * r, 128 * r + 128), V("IDB"), scale=V("EQ", r, r + 1))
 
-    def argmax(b, w):
-        o, kp = 128 * b, V("KP%d" % b, 0, 128)
-        o1, q = o + 128, 144 * b
-        f, em, am, bm, y, st, de = (V(x, o, o1) for x in ("F", "EM", "AM", "BM", "Y", "ST", "DE"))
-        scan(f, V("RST"), kp, THR, A.min, A.max)
-        tt(em, kp, f, A.is_equal)
-        tt(am, ZMP, em, A.is_gt)
-        tt(bm, em, st, A.mult)
-        scan(y, am, bm, 0.0, A.mult, A.add)
-        tt(V("D", q, q + 128), y, SELP, A.mult)
-        scan(V("R", q, q + 143), V("Z3"), V("D", q, q + 143), 0.0, A.mult, A.add)
-        tt(de, V("R", q + 15, q + 143), M16P, A.mult)
-        mm(V("LP", 8 * b, 8 * b + w // 16), de, V("Q%d" % b, 0, w // 16), True, True)
-        mm(V("ROW", o, o + w), V("R", q + 15, q + 143), V(("IDF", "ID1")[b], 0, w), True, True)
+    def argmax(b):
+        o, o1, kp = 128 * b, 128 * b + 128, V("KP%d" % b, 0, 128)
+        f, em, am, y, st = (V(x, o, o1) for x in ("F", "EM", "AM", "Y", "ST"))
+        bm = V("ST", 256 + o, 256 + o1)
+        yield lambda: scan(f, V("RST"), kp, THR, A.min, A.max)
+        yield lambda: tt(em, kp, f, A.is_equal)
+        yield lambda: tt(am, ZMP, em, A.is_gt)
+        yield lambda: tt(bm, em, st, A.mult)
+        yield lambda: scan(y, am, bm, 0.0, A.mult, A.add)
+
+    def spread(bs, L):
+        o, n = 128 * bs[0], 128 * len(bs)
+        cp(V("D", o + 15, o + n, 16), V("Y", o + 15, o + n, 16))
+        scan(V("R", o + 15, o + n + 15), V("Z3", 15, n + 15), V("D", o + 15, o + n + 15), 0.0, A.mult, A.add)
+        ws = [(b, 128 * b, min(128, L - 128 * b)) for b in bs]
+        for b, p, w in ws:
+            mm(V("ROW", p, p + w), V("R", p + 15, p + 143), V(("IDF", "ID1")[b], 0, w), True, True)
+        tt(V("DE", o, o + n), V("R", o + 15, o + n + 15), V("CON", 128, 128 + n), A.mult)
+        for b, p, w in ws:
+            mm(V("LP", 8 * b, 8 * b + w // 16), V("DE", p, p + 128), V("Q%d" % b, 0, w // 16), True, True)
 
     def step(u):
         t, e = divmod(u, 2)
@@ -238,8 +256,10 @@ def rank_program(g, core, T, topo):
         for b in range(nb):
             for (po, m, c0) in [(0, 128, xs[0][2])] if b == 0 else [(96, 32, ent + 128), (0, 96, PAD + 1888)]:
                 out = V("ST", 128 * b, 128 * b + 128, p=(po, po + m))
-                mm(out, V("ONEF", 0, m, p=(0, 1)), V("PB", p=(0, 1)), True, False)
-                mm(out, V("S", c0, c0 + m), V("IDF"), False, True)
+                none = u == 0 and m == 96
+                mm(out, V("ONEB", 0, m, p=(0, 1)), V("PB", p=(0, 1)), True, none)
+                if not none:
+                    mm(out, V("S", c0, c0 + m), V("IDF"), False, True)
         if u == 0:
             mm(V("KP1", 0, 128, p=(0, 96)), V("ONEB", 0, 96, p=(0, 1)), V("KB", p=(0, 1)), True, True)
         for (l0, l1) in chunks:
@@ -256,19 +276,27 @@ def rank_program(g, core, T, topo):
                     for k in range(16):
                         mm(V("KP%d" % b, k, 128, 16, p=(po, po + m)), V("MN", 16 * bl + k, 16 * (bl + m - 1) + k + 1, 16),
                            V("SW16"), False, k == 15)
-        for f in late:
-            f()
+        ready = [f() for f in late]
         late.clear()
-        if u == 0:
-            consts_on_scalar()
         for (lo, hi, cb, cc, sb, so) in cs:
             act(V("CPB", lo, hi), V(cb, cc, cc + hi - lo))
-        for b in range(nb):
-            argmax(b, min(128, L - 128 * b))
-        lp, yo, l3 = V("LP", 0, h), V("YO16", 0, h), V("L3F", 0, h)
-        cp(yo, lp)
+        if u == 0:
+            consts_on_scalar()
+            mix(*ready)
+            mix(argmax(0), argmax(1))
+            spread((0, 1), L)
+        elif e:
+            mix(*ready)
+            mix(argmax(0))
+            spread((0,), L)
+        else:
+            mix(*ready, argmax(0))
+            spread((0,), L)
+            mix(argmax(1))
+            spread((1,), L)
+        l3, yo = V("LP", 0, h), V("YO16", 0, h)
         cp(V("YU", 0, L), V("ROW", 0, L))
-        cp(l3, yo)
+        cp(yo, l3)
         lv = V("LV", 0, L)
         act(lv, V("ROW", 0, L), AF.Sign, scale=-1.0)
         cg, sg = V("CG", 0, L), V("SG", 0, L)
@@ -277,20 +305,21 @@ def rank_program(g, core, T, topo):
         op("qs", lambda: g.scalar.activation(sg[0], swin[0].indirect(yo[0]), AF.Copy), [sg], [swin, yo])
         mm(V("DUP", 0, L), V("BONES"), lv, True, False)
         for q in range(h):
-            ts(V("E", 256 * q, 256 * q + L - 16 * q), V("YU", 16 * q, L), V("L3F", q, q + 1), A.is_equal)
+            ts(V("E", 256 * q, 256 * q + L - 16 * q), V("YU", 16 * q, L), V("LP", q, q + 1), A.is_equal)
             if q < h - 1:
                 mm(V("DUP", 16 * q + 16, L), V("BONES"), V("E", 256 * q + 16, 256 * q + L - 16 * q), False, False)
         for c in range(1, 16):
             mm(V("DUP", c, L, 16), V("TRI", 128 * c, 128 * c + 128), V("E", c, 256 * (h - 1) + c + 1, 256), False, c == 15)
-        for b in range(nb):
-            tt(V("WB", 128 * b, 128 * b + 128), V("ST", 128 * b, 128 * b + 128), V("R", 144 * b + 15, 144 * b + 143), A.is_equal)
-        m = V("MM", 0, L)
-        tt(m, cg, V("CPB", 0, L), A.min)
+        tt(V("WB", 0, 128 * nb), V("ST", 256, 256 + 128 * nb), V("R", 15, 15 + 128 * nb), A.is_equal)
+        w = V("WW", 0, h)
+        tt(w, V("DUMPY", 0, h), l3, A.subtract)
         stn, ds, rk = V("CPB", 256, 256 + L), V("DS", 0, L), V("RK", 0, L)
         ts(stn, V("DUP", 0, L), -16.0, A.is_equal, -1.0, A.mult)
         scan(ds, stn, V("ZERO", 0, L), 129.0, A.add, A.max)
         tt(rk, ds, stn, A.mult)
-        rp = V("LP", 16, 16 + h)
+        m = V("MM", 0, L)
+        tt(m, cg, V("CPB", 0, L), A.min)
+        rp = V("LP", h, 2 * h)
         for r in range(16):
             mm(rp, V("SEL", 128 * r, 128 * r + 128), V("RK", r, L, 16), r == 0, r == 15)
         for b, x in enumerate((128,) if e else (128, L - 128)):
@@ -298,17 +327,13 @@ def rank_program(g, core, T, topo):
         kr, kn = V("KR", 0, L), V("CPB", 256, 256 + L)
         act(kr, rk, AF.Sign, scale=-1.0)
         act(kn, kr, AF.Copy, scale=float(n0 + 128))
-        w = V("WW", 0, h)
-        tt(w, V("DUMPY", 0, h), l3, A.subtract)
-        dm = V("DM", 0, h)
-        xn, xy = V("X", 0, h), V("X", h, 2 * h)
+        dm, x = V("DM", 0, h), V("X", 0, 2 * h)
         ts(dm, rp, 0.0, A.is_equal)
-        tt(xn, dm, V("DUMPN", 16 * u, 16 * u + h), A.mult)
-        tt(xy, dm, w, A.mult)
-        tt(xn, xn, rp, A.add)
-        tt(xy, xy, l3, A.add)
-        ts(V("X16", 0, 2 * h), V("X", 0, 2 * h), 128.0, A.add)
-        on, oy = V("X16", 0, h), V("X16", h, 2 * h)
+        tt(V("X", 0, h), dm, w, A.mult)
+        tt(V("X", h, 2 * h), dm, V("DUMPN", 16 * u, 16 * u + h), A.mult)
+        tt(x, x, V("LP", 0, 2 * h), A.add)
+        ts(V("X16", 0, 2 * h), x, 128.0, A.add)
+        oy, on = V("X16", 0, h), V("X16", h, 2 * h)
         op("qv", lambda: g.vector.tensor_copy(T.C[:, a:CW].indirect(on[0]), m[0]), [V("C", a, CW)], [on, m])
         op("qv", lambda: g.vector.tensor_tensor(T.C[:].indirect(oy[0]), cg[0], m[0], A.subtract), [V("C")], [oy, cg, m])
         if u == 5:
@@ -318,16 +343,20 @@ def rank_program(g, core, T, topo):
             cp(V("S16N"), V("S", a, a + 128))
 
         def links():
-            tt(V("NK", 0, L), kn, rk, A.add)
-            tt(kn, V("NK", 0, L), V("ROW", 256, 256 + L), A.mult)
+            yield lambda: tt(V("NK", 0, L), kn, rk, A.add)
+            yield lambda: tt(kn, V("NK", 0, L), V("ROW", 256, 256 + L), A.mult)
             for (lo, hi, c) in xs:
-                x = V("S", c, c + hi - lo)
-                tt(x, x, V("CPB", 256 + lo, 256 + hi), A.max)
+                x, y = V("S", c, c + hi - lo), V("CPB", 256 + lo, 256 + hi)
+                yield lambda: tt(x, x, y, A.max)
             if u == 2:
-                cp(V("S16E", 480, 576), V("S", PAD + 1888, PAD + 1984))
+                yield lambda: cp(V("S16E", 480, 576), V("S", PAD + 1888, PAD + 1984))
             if u == 4:
                 dma("sync", T.ys[:, 0:1088], T.S[:, PAD + 1408:PAD + 2496], [], [V("S", PAD + 1408, PAD + 2496)])
-        late.append(links)
+        chain = links()
+        if e and u < 5:
+            for i in range(2):
+                next(chain)()
+        late.append(lambda: chain)
 
         if e == 1 and t < 2:
             nxt, prv = T.cores[(rank + 1) % len(T.cores)], T.cores[(rank - 1) % len(T.cores)]
@@ -342,7 +371,7 @@ def rank_program(g, core, T, topo):
 
     for u in range(6):
         step(u)
-    late[0]()
+    mix(late[0]())
     dma("sync", T.ys[:, 1088:1344], T.S[:, PAD + 2496:COL], [], [V("S", PAD + 2496, COL)])
     for s in range(dmas[0]):
         g.sync.wait_ge(T.sem[DSEMS[s]], 16)

from concourse.mybir import dt, AluOpType, ActivationFunctionType

PAD = 136
NV = 2752
COL = PAD + NV
DSZ = 368
CW = COL + 2 * DSZ
SW = COL + DSZ
THR = 524287.5

F32, BF, I32, U16 = "float32", "bfloat16", "int32", "uint16"
SCRATCH = {
    "C": ("sbuf", [128, CW], F32), "S": ("sbuf", [128, SW], F32),
    "CL": ("sbuf", [128, 1984], I32), "SL": ("sbuf", [128, 1984], I32),
    "S16E": ("sbuf", [128, 576], U16), "S16N": ("sbuf", [128, 128], U16),
    "P1": ("sbuf", [128, 96], F32), "P2": ("sbuf", [128, 96], F32),
    "CX": ("sbuf", [128, 4096], F32), "MN": ("sbuf", [128, 4096], F32),
    "REPI": ("sbuf", [128, 64], I32), "REPL": ("sbuf", [128, 64], U16),
    "PI": ("sbuf", [128, 1], I32), "PA": ("sbuf", [128, 1], I32), "PM": ("sbuf", [128, 1], F32),
    "IR": ("sbuf", [128, 128], F32),
    "ONEF": ("sbuf", [128, 128], F32), "ONEB": ("sbuf", [128, 128], BF),
    "IDF": ("sbuf", [128, 128], F32), "ID1": ("sbuf", [128, 128], F32),
    "IDB": ("sbuf", [128, 128], BF), "IB1": ("sbuf", [128, 128], BF),
    "BA": ("sbuf", [128, 128], BF), "BONES": ("sbuf", [128, 128], BF),
    "TC": ("sbuf", [128, 16], F32), "EQ": ("sbuf", [128, 16], F32),
    "TRI": ("sbuf", [128, 2048], BF), "SEL": ("sbuf", [128, 2048], BF),
    "SW0": ("sbuf", [128, 8], F32), "SW1": ("sbuf", [128, 8], F32), "SW16": ("sbuf", [128, 8], F32),
    "Q0": ("sbuf", [128, 8], F32), "Q1": ("sbuf", [128, 8], F32),
    "KB": ("sbuf", [128, 128], BF), "PB": ("sbuf", [128, 128], BF), "RST": ("sbuf", [128, 128], F32),
    "Z3": ("sbuf", [128, 272], F32), "ZERO": ("sbuf", [128, 256], F32),
    "DUMPY": ("sbuf", [128, 16], F32), "DUMPN": ("sbuf", [128, 96], F32),
    "F": ("sbuf", [128, 256], F32), "EM": ("sbuf", [128, 256], F32), "AM": ("sbuf", [128, 256], F32),
    "Y": ("sbuf", [128, 256], F32), "DE": ("sbuf", [128, 256], F32),
    "D": ("sbuf", [128, 272], F32), "R": ("sbuf", [128, 272], F32), "WB": ("sbuf", [128, 256], BF),
    "YO16": ("sbuf", [128, 16], U16),
    "YU": ("sbuf", [128, 256], U16), "LV": ("sbuf", [128, 256], BF), "E": ("sbuf", [128, 4096], BF),
    "CG": ("sbuf", [128, 256], F32), "SG": ("sbuf", [128, 256], F32),
    "MM": ("sbuf", [128, 256], F32), "WW": ("sbuf", [128, 16], F32),
    "DS": ("sbuf", [128, 256], F32), "RK": ("sbuf", [128, 256], BF), "DM": ("sbuf", [128, 16], F32),
    "X": ("sbuf", [128, 32], F32), "X16": ("sbuf", [128, 32], U16),
    "KR": ("sbuf", [128, 256], F32), "NK": ("sbuf", [128, 256], F32),
    "KP0": ("psum", [128, 512], F32), "KP1": ("psum", [128, 512], F32), "ST": ("psum", [128, 512], F32),
    "CON": ("psum", [128, 512], F32), "ROW": ("psum", [128, 512], F32), "DUP": ("psum", [128, 512], F32),
    "CPB": ("psum", [128, 512], F32), "LP": ("psum", [128, 512], F32),
}
QUEUES = ("qv", "qs", "qt", "qp")
DSEMS = ["dm%d" % i for i in range(12)]
SEMAPHORES = list(QUEUES) + DSEMS + ["snd1", "snd2", "arr1", "arr2"]
PSUM = {n for n in SCRATCH if SCRATCH[n][0] == "psum"}


def rank_program(g, core, T, topo):
    rank = T.rank_of(core)
    if rank is None:
        return
    A, AF = AluOpType, ActivationFunctionType
    eng = {"qv": g.vector, "qs": g.scalar, "qt": g.tensor, "qp": g, "sync": g.sync}
    cnt, known, log, dmas = {}, {}, {}, [0]

    def V(name, a=0, b=None, st=1, p=None):
        n = SCRATCH[name][1][1]
        b = n if b is None else b
        t = T[name]
        x = t[:, a:b:st] if p is None else t[p[0]:p[1], a:b:st]
        return (x, name, a, b)

    def need(q, w, r):
        dep = {}
        for views, wr in ((w, True), (r, False)):
            for (_, name, a, b) in views:
                ps = name in PSUM
                for (lo, hi, ww, e, c) in log.get(name, ()):
                    other = ps and e != q
                    if not other and (hi <= a or b <= lo or not (wr or ww)):
                        continue
                    if ps and e == q == "qt":
                        continue
                    dep[e] = max(dep.get(e, 0), c)
        for e in sorted(dep):
            if known.get((q, e), 0) < dep[e]:
                known[(q, e)] = dep[e]
                eng[q].wait_ge(T.sem[e], dep[e])

    def note(tok, w, r):
        for views, wr in ((w, True), (r, False)):
            for (_, name, a, b) in views:
                ls = log.setdefault(name, [])
                if wr:
                    ls[:] = [x for x in ls if not (a <= x[0] and x[1] <= b)]
                ls.append((a, b, wr, tok[0], tok[1]))

    def op(q, fn, w, r):
        need(q, w, r)
        cnt[q] = cnt.get(q, 0) + 1
        fn().then_inc(T.sem[q], 1)
        note((q, cnt[q]), w, r)

    def dma(q, out, in_, w, r):
        need(q, w, r)
        s = DSEMS[dmas[0]]
        dmas[0] += 1
        eng[q].dma_start(out, in_).then_inc(T.sem[s], 16)
        note((s, 16), w, r)

    def tt(out, a, b, o):
        op("qv", lambda: g.vector.tensor_tensor(out[0], a[0], b[0], o), [out], [a, b])

    def ts(out, a, s, o, s2=None, o2=None):
        sc, rd = (s[0], [a, s]) if isinstance(s, tuple) else (s, [a])
        if o2 is None:
            op("qv", lambda: g.vector.tensor_scalar(out[0], a[0], sc, None, o), [out], rd)
        else:
            op("qv", lambda: g.vector.tensor_scalar(out[0], a[0], sc, s2, o, o2), [out], rd)

    def cp(out, a):
        op("qv", lambda: g.vector.tensor_copy(out[0], a[0]), [out], [a])

    def scan(out, a, b, ini, o1, o2):
        op("qv", lambda: g.vector.tensor_tensor_scan(out[0], a[0], b[0], ini, o1, o2), [out], [a, b])

    def fill(out, c):
        op("qv", lambda: g.vector.memset(out[0], c), [out], [])

    def act(out, a, f=AF.Copy, **k):
        rd = [a] + [x for x in k.values() if isinstance(x, tuple)]
        kk = {n: (x[0] if isinstance(x, tuple) else x) for n, x in k.items()}
        op("qs", lambda: g.scalar.activation(out[0], a[0], f, **kk), [out], rd)

    def mm(out, l, r, start, stop):
        op("qt", lambda: g.tensor.matmul(out[0], l[0], r[0], start, stop), [out], [l, r])

    def iota(out, pat, base, cm):
        op("qp", lambda: g.iota(out[0], pat, base, cm, allow_small_or_imprecise_dtypes=True), [out], [])

    def asel(out, a, pat, o, base, cm):
        op("qp", lambda: g.affine_select(out[0], a[0], pat, o, 0.0, base, cm), [out], [a])

    def mix(*chains):
        chains = [iter(c) for c in chains]
        while chains:
            for c in list(chains):
                f = next(c, None)
                if f is None:
                    chains.remove(c)
                else:
                    f()

    dma("sync", T.SL[:, 1408:1568], T.s0[:, 1408:1568], [V("SL", 1408, 1568)], [])
    dma("qs", T.CL[:, 1408:1984], T.c0[:, 1408:1984], [V("CL", 1408, 1984)], [])
    dma("sync", T.CL[:, 0:704], T.c0[:, 0:704], [V("CL", 0, 704)], [])
    dma("qs", T.CL[:, 704:1408], T.c0[:, 704:1408], [V("CL", 704, 1408)], [])
    dma("sync", T.SL[:, 1568:1984], T.s0[:, 1568:1984], [V("SL", 1568, 1984)], [])
    dma("sync", T.SL[:, 0:1408], T.s0[:, 0:1408], [V("SL", 0, 1408)], [])

    fill(V("ONEB"), 1.0)
    fill(V("ONEF"), 1.0)
    fill(V("SW0"), 16.0)
    iota(V("REPI"), [[1, 64]], 0, 0)
    iota(V("PI"), [[1, 1]], 0, 1)
    iota(V("IR"), [[0, 8], [1, 16]], 0, 0)
    asel(V("BA"), V("ONEB"), [[-16, 8], [0, 16]], A.is_ge, 0, 1)
    asel(V("BONES"), V("BA"), [[16, 8], [0, 16]], A.is_ge, 15, -1)
    asel(V("SW1"), V("SW0"), [[-16, 8]], A.is_ge, 0, 1)
    asel(V("SW16"), V("SW1"), [[16, 8]], A.is_ge, 15, -1)
    asel(V("IDF"), V("ONEF"), [[-1, 128]], A.is_equal, 0, 1)
    iota(V("C", 128, 136), [[0, 8]], 0, 0)
    iota(V("C", 2120, COL), [[0, 768]], 0, 0)
    iota(V("S", 128, 136), [[0, 8]], 0, 0)
    iota(V("S", 2120, COL), [[0, 768]], 0, 0)
    iota(V("DUMPY"), [[16, 16]], COL + DSZ - 128, 1)
    for u in range(6):
        iota(V("DUMPN", 16 * u, 16 * u + 16), [[16, 16]], COL - 128 - (PAD + 1984 + 128 * u), 1)
    cp(V("REPL"), V("REPI"))
    ts(V("PA"), V("PI"), 15, A.bitwise_and)
    cp(V("PM"), V("PA"))
    ts(V("KB"), V("IR"), -1.0, A.mult, 15.0, A.add)
    fill(V("PB"), 8.0)
    ZMP = V("CON", 0, 128)
    ts(ZMP, V("IR"), 0.0, A.is_gt)
    ts(V("CON", 128, 256), V("IR"), V("PM"), A.is_equal)
    ts(V("CON", 256, 384), V("IR"), V("PM"), A.is_equal)
    ts(V("RST"), V("IR"), 0.0, A.is_gt, 33554432.0, A.mult)
    ts(V("RST"), V("RST"), THR, A.max)
    fill(V("Z3"), 1.0)
    fill(V("Z3", 15, 272, 16), 0.0)
    fill(V("D"), 0.0)
    fill(V("ZERO"), 0.0)
    ts(V("TC"), V("IR", 0, 16), V("PM"), A.is_gt)
    ts(V("EQ"), V("IR", 0, 16), V("PM"), A.is_equal)

    cp(V("S16E", 0, 160), V("SL", 1408, 1568))
    cp(V("C", PAD + 1408, PAD + 1568), V("CL", 1408, 1568))
    cp(V("S", PAD + 1408, PAD + 1568), V("SL", 1408, 1568))
    cp(V("C", PAD + 1568, PAD + 1984), V("CL", 1568, 1984))
    cp(V("C", PAD, PAD + 704), V("CL", 0, 704))

    def more():
        yield lambda: cp(V("C", PAD + 704, PAD + 1408), V("CL", 704, 1408))
        yield lambda: cp(V("S16E", 160, 576), V("SL", 1568, 1984))
        yield lambda: cp(V("S", PAD + 1568, PAD + 1984), V("SL", 1568, 1984))
        yield lambda: cp(V("S", PAD, PAD + 1408), V("SL", 0, 1408))
    late = [more]

    def consts_on_scalar():
        act(V("Q0"), V("SW16"), scale=0.0625)
        act(V("Q1", 0, 2), V("Q0", 6, 8))
        act(V("Q1", 2, 8), V("Q0", 0, 6))
        act(V("ID1", 0, 32), V("IDF", 96, 128))
        act(V("ID1", 32, 128), V("IDF", 0, 96))
        act(V("IDB"), V("IDF"))
        act(V("IB1"), V("ID1"))
        for c in range(1, 16):
            act(V("TRI", 128 * c, 128 * c + 128), V("BONES"), scale=V("TC", c, c + 1))
        for r in range(16):
            act(V("SEL", 128 * r, 128 * r + 128), V("IDB"), scale=V("EQ", r, r + 1))

    def argmax(b):
        o, o1, kp = 128 * b, 128 * b + 128, V("KP%d" % b, 0, 128)
        f, em, am, y, st = (V(x, o, o1) for x in ("F", "EM", "AM", "Y", "ST"))
        bm = V("ST", 256 + o, 256 + o1)
        yield lambda: scan(f, V("RST"), kp, THR, A.min, A.max)
        yield lambda: tt(em, kp, f, A.is_equal)
        yield lambda: tt(am, ZMP, em, A.is_gt)
        yield lambda: tt(bm, em, st, A.mult)
        yield lambda: scan(y, am, bm, 0.0, A.mult, A.add)

    def spread(bs, L):
        o, n = 128 * bs[0], 128 * len(bs)
        cp(V("D", o + 15, o + n, 16), V("Y", o + 15, o + n, 16))
        scan(V("R", o + 15, o + n + 15), V("Z3", 15, n + 15), V("D", o + 15, o + n + 15), 0.0, A.mult, A.add)
        ws = [(b, 128 * b, min(128, L - 128 * b)) for b in bs]
        for b, p, w in ws:
            mm(V("ROW", p, p + w), V("R", p + 15, p + 143), V(("IDF", "ID1")[b], 0, w), True, True)
        tt(V("DE", o, o + n), V("R", o + 15, o + n + 15), V("CON", 128, 128 + n), A.mult)
        for b, p, w in ws:
            mm(V("LP", 8 * b, 8 * b + w // 16), V("DE", p, p + 128), V("Q%d" % b, 0, w // 16), True, True)

    def step(u):
        t, e = divmod(u, 2)
        nb = 2 - e
        L = (256 if t else 160) if e == 0 else 128
        h, n0 = L // 16, 1984 + 128 * u
        a = PAD + n0
        ent = PAD + 1408 + 160 * t
        ports = "P%d" % t
        if e == 0:
            xs = [(0, 160, ent)] + ([(160, 256, PAD + 1888)] if t else [])
            cs = [(0, 160, "C", ent, "S16E", 160 * t)] + ([(160, 256, ports, 0, "S16E", 480)] if t else [])
            blocks = [(0, 0, 128, 0), (128, 96, 32, 1)] + ([(160, 0, 96, 1)] if t else [])
            chunks = [(0, 16), (16, 48), (48, 88), (88, 128), (128, 160)] + ([(160, 208), (208, 256)] if t else [])
        else:
            xs = [(0, 128, a - 128)]
            cs = [(0, 128, "C", a - 128, "S16N", 0)]
            blocks = [(0, 0, 128, 0)]
            chunks = [(0, 32), (32, 64), (64, 96), (96, 128)]
        for b in range(nb):
            for (po, m, c0) in [(0, 128, xs[0][2])] if b == 0 else [(96, 32, ent + 128), (0, 96, PAD + 1888)]:
                out = V("ST", 128 * b, 128 * b + 128, p=(po, po + m))
                none = u == 0 and m == 96
                mm(out, V("ONEB", 0, m, p=(0, 1)), V("PB", p=(0, 1)), True, none)
                if not none:
                    mm(out, V("S", c0, c0 + m), V("IDF"), False, True)
        if u == 0:
            mm(V("KP1", 0, 128, p=(0, 96)), V("ONEB", 0, 96, p=(0, 1)), V("KB", p=(0, 1)), True, True)
        for (l0, l1) in chunks:
            lo, hi, cb, cc, sb, so = [x for x in cs if x[0] <= l0 < x[1]][0]
            src = V(cb, cc + l0 - lo, cc + l1 - lo)
            rep, off = V("REPL", 0, l1 - l0), V(sb, so + l0 - lo, so + l1 - lo)
            cx, mn = V("CX", 16 * l0, 16 * l1), V("MN", 16 * l0, 16 * l1)
            op("qs", lambda: g.scalar.activation(cx[0], src[0].indirect(rep[0]), AF.Copy), [cx], [src, rep])
            win = V("CL") if u == 0 else V("C", PAD, COL)
            op("qv", lambda: g.vector.tensor_tensor(mn[0], win[0].indirect(off[0]), cx[0], A.min), [mn], [win, off, cx])
            for (bl, po, m, b) in blocks:
                if bl + m == l1:
                    mm(V("KP%d" % b, 0, 128, p=(po, po + m)), V("ONEB", 0, m, p=(0, 1)), V("KB", p=(0, 1)), True, False)
                    for k in range(16):
                        mm(V("KP%d" % b, k, 128, 16, p=(po, po + m)), V("MN", 16 * bl + k, 16 * (bl + m - 1) + k + 1, 16),
                           V("SW16"), False, k == 15)
        ready = [f() for f in late]
        late.clear()
        for (lo, hi, cb, cc, sb, so) in cs:
            act(V("CPB", lo, hi), V(cb, cc, cc + hi - lo))
        if u == 0:
            consts_on_scalar()
            mix(*ready)
            mix(argmax(0), argmax(1))
            spread((0, 1), L)
        elif e:
            mix(*ready)
            mix(argmax(0))
            spread((0,), L)
        else:
            mix(*ready, argmax(0))
            spread((0,), L)
            mix(argmax(1))
            spread((1,), L)
        l3, yo = V("LP", 0, h), V("YO16", 0, h)
        cp(V("YU", 0, L), V("ROW", 0, L))
        cp(yo, l3)
        lv = V("LV", 0, L)
        act(lv, V("ROW", 0, L), AF.Sign, scale=-1.0)
        cg, sg = V("CG", 0, L), V("SG", 0, L)
        cwin, swin = V("C", 128, COL), V("S", 128, COL)
        op("qs", lambda: g.scalar.activation(cg[0], cwin[0].indirect(yo[0]), AF.Copy), [cg], [cwin, yo])
        op("qs", lambda: g.scalar.activation(sg[0], swin[0].indirect(yo[0]), AF.Copy), [sg], [swin, yo])
        mm(V("DUP", 0, L), V("BONES"), lv, True, False)
        for q in range(h):
            ts(V("E", 256 * q, 256 * q + L - 16 * q), V("YU", 16 * q, L), V("LP", q, q + 1), A.is_equal)
            if q < h - 1:
                mm(V("DUP", 16 * q + 16, L), V("BONES"), V("E", 256 * q + 16, 256 * q + L - 16 * q), False, False)
        for c in range(1, 16):
            mm(V("DUP", c, L, 16), V("TRI", 128 * c, 128 * c + 128), V("E", c, 256 * (h - 1) + c + 1, 256), False, c == 15)
        tt(V("WB", 0, 128 * nb), V("ST", 256, 256 + 128 * nb), V("R", 15, 15 + 128 * nb), A.is_equal)
        w = V("WW", 0, h)
        tt(w, V("DUMPY", 0, h), l3, A.subtract)
        stn, ds, rk = V("CPB", 256, 256 + L), V("DS", 0, L), V("RK", 0, L)
        ts(stn, V("DUP", 0, L), -16.0, A.is_equal, -1.0, A.mult)
        scan(ds, stn, V("ZERO", 0, L), 129.0, A.add, A.max)
        tt(rk, ds, stn, A.mult)
        m = V("MM", 0, L)
        tt(m, cg, V("CPB", 0, L), A.min)
        rp = V("LP", h, 2 * h)
        for r in range(16):
            mm(rp, V("SEL", 128 * r, 128 * r + 128), V("RK", r, L, 16), r == 0, r == 15)
        for b, x in enumerate((128,) if e else (128, L - 128)):
            mm(V("ROW", 256 + 128 * b, 256 + 128 * b + x), V("WB", 128 * b, 128 * b + 128), V(("IDB", "IB1")[b], 0, x), True, True)
        kr, kn = V("KR", 0, L), V("CPB", 256, 256 + L)
        act(kr, rk, AF.Sign, scale=-1.0)
        act(kn, kr, AF.Copy, scale=float(n0 + 128))
        dm, x = V("DM", 0, h), V("X", 0, 2 * h)
        ts(dm, rp, 0.0, A.is_equal)
        tt(V("X", 0, h), dm, w, A.mult)
        tt(V("X", h, 2 * h), dm, V("DUMPN", 16 * u, 16 * u + h), A.mult)
        tt(x, x, V("LP", 0, 2 * h), A.add)
        ts(V("X16", 0, 2 * h), x, 128.0, A.add)
        oy, on = V("X16", 0, h), V("X16", h, 2 * h)
        op("qv", lambda: g.vector.tensor_copy(T.C[:, a:CW].indirect(on[0]), m[0]), [V("C", a, CW)], [on, m])
        op("qv", lambda: g.vector.tensor_tensor(T.C[:].indirect(oy[0]), cg[0], m[0], A.subtract), [V("C")], [oy, cg, m])
        if u == 5:
            dma("sync", T.yc[:, :], T.C[:, PAD:COL], [], [V("C", PAD, COL)])
        op("qv", lambda: g.vector.tensor_copy(T.S[:, a:SW].indirect(on[0]), sg[0]), [V("S", a, SW)], [on, sg])
        if e == 0:
            cp(V("S16N"), V("S", a, a + 128))

        def links():
            yield lambda: tt(V("NK", 0, L), kn, rk, A.add)
            yield lambda: tt(kn, V("NK", 0, L), V("ROW", 256, 256 + L), A.mult)
            for (lo, hi, c) in xs:
                x, y = V("S", c, c + hi - lo), V("CPB", 256 + lo, 256 + hi)
                yield lambda: tt(x, x, y, A.max)
            if u == 2:
                yield lambda: cp(V("S16E", 480, 576), V("S", PAD + 1888, PAD + 1984))
            if u == 4:
                dma("sync", T.ys[:, 0:1088], T.S[:, PAD + 1408:PAD + 2496], [], [V("S", PAD + 1408, PAD + 2496)])
        chain = links()
        if e and u < 5:
            for i in range(2):
                next(chain)()
        late.append(lambda: chain)

        if e == 1 and t < 2:
            nxt, prv = T.cores[(rank + 1) % len(T.cores)], T.cores[(rank - 1) % len(T.cores)]
            rid, pid = topo.addr(nxt)[:2]
            me, got = topo.engines(core, nxt)[:8], len(topo.engines(prv, core)[:8])
            src, dst = V("C", a, a + 96), V("P%d" % (t + 1))
            snd, arr = "snd%d" % (t + 1), "arr%d" % (t + 1)
            need("qp", [], [src])
            g.remote_dma(dst[0], src[0], T.sem[arr], T.sem[snd], pid, rid, sum(1 << i for i in me))
            note((snd, len(me)), [], [src])
            note((arr, got), [dst], [])

    for u in range(6):
        step(u)
    mix(late[0]())
    dma("sync", T.ys[:, 1088:1344], T.S[:, PAD + 2496:COL], [], [V("S", PAD + 2496, COL)])
    for s in range(dmas[0]):
        g.sync.wait_ge(T.sem[DSEMS[s]], 16)
    for q in QUEUES:
        g.sync.wait_ge(T.sem[q], cnt[q])
